import numpy as np, ml_dtypes
CORES = [5,29,101,125,133,157,229,253]
N = 8
GR, GC, TK = 4, 2, 512
RA = [[2,2,-2,2],[-2,-2,-2,-1],[-2,-2,2,2],[2,-1,1,1]]
CB = [[2,-1],[-1,-1]]
def setup_inputs(rng):
    return {"x": rng.standard_normal((N, 128, TK), dtype=np.float32).astype(ml_dtypes.bfloat16), "a": (rng.standard_normal((N, 128, 128), dtype=np.float32) / 11).astype(ml_dtypes.bfloat16)}
def setup_inputs_big(rng):
    d = setup_inputs(rng)
    for k in ("x", "a"): d[k] = (d[k].astype(np.float32) * 1024.0).astype(d[k].dtype)
    return d
def setup_inputs_small(rng):
    d = setup_inputs(rng)
    for k in ("x", "a"): d[k] = (d[k].astype(np.float32) * (1 / 1024.0)).astype(d[k].dtype)
    return d
def setup_inputs_apart(rng):
    d = setup_inputs(rng)
    f = (10.0 ** rng.permutation(np.linspace(-1.5, 1.5, N))).astype(np.float32).reshape(N, 1, 1)
    for k in ("x", "a"): d[k] = (d[k].astype(np.float32) * f).astype(d[k].dtype)
    return d
def reference(x, a):
    X, A = x.astype(np.float64), a.astype(np.float64)
    y = np.zeros((N, 128, TK))
    for i in range(GR):
        for j in range(GC):
            t = sum(RA[i][k] * CB[j][l] * X[k * GC + l] for k in range(GR) for l in range(GC))
            y[i * GC + j] = A[i * GC + j].T @ t
    return {"y": y.astype(ml_dtypes.bfloat16)}

@@ -1,0 +1,148 @@
+from concourse.bass import DstId, RemoteDMATransfer
+from concourse.mybir import AluOpType
+
+WORLD = 256
+GR, GC, W, M = 4, 2, 512, 128
+
+SCRATCH = {
+    "land": ("sbuf", [128, 4 * W], "bfloat16"),
+    "out": ("sbuf", [128, W], "bfloat16"),
+    "a0": ("sbuf", [128, M], "bfloat16"),
+    "cst": ("sbuf", [128, 4 * M], "bfloat16"),
+    "asc": ("sbuf", [128, 4 * M], "bfloat16"),
+    "rs": ("sbuf", [128, 2 * W], "float32"),
+    "pa": ("psum", [128, W], "float32"),
+    "pb": ("psum", [128, W], "float32"),
+}
+SEMAPHORES = ["ldx", "lda", "fill", "ascd", "mm", "cp", "st", "sent", "vs",
+              "xa0", "xa1", "xa2", "xa3", "xpar", "vown", "vcross"]
+OWN_X, PAR_X, OWN_W, CROSS_W = 0, 1, 2, 3
+
+
+def _count(mask):
+    return bin(mask).count("1")
+
+
+def _plan(RA, i):
+    order = [(i - d) % GR for d in range(1, GR)]
+    steps, s = [], RA[i][order[0]]
+    for k in order[1:]:
+        c = RA[i][k]
+        if abs(c) != abs(s):
+            f = abs(s) / abs(c)
+            steps.append(("scale", f))
+            s = s / f
+        steps.append(("add" if c == s else "sub", k))
+    return order, steps, s
+
+
+def _combiner(topo, R, P):
+    c = [c for c in range(WORLD) if c != R and topo.host(c) == topo.host(R) and topo.chip(c) == topo.chip(R)
+         and topo.may_write(c, P)]
+    return sorted(c, key=lambda c: (topo.die(c) != topo.die(R), c))[0]
+
+
+def _slot(T, q):
+    return T.land[:, q * W:(q + 1) * W]
+
+
+def rank_program(g, core, T, topo):
+    RA, CB = T.tables["RA"], T.tables["CB"]
+    rank_at = lambda i, l: T.cores[i * GC + l]
+    comb = {(i, l): _combiner(topo, rank_at(i, l), rank_at(i, 1 - l)) for i in range(GR) for l in range(GC)}
+    xa = [T.sem["xa%d" % k] for k in range(GR)]
+
+    def send(dst, out_ap, in_ap, sem, mask):
+        rid, pid = topo.addr(dst, core)
+        g.remote_dma(out_ap=out_ap, in_ap=in_ap, remote_sem=sem, local_sem=T.sem.sent, pid=pid, routing_id=rid,
+                     dma_engine_mask=mask)
+        return _count(mask)
+
+    rank = T.rank_of(core)
+    if rank is not None:
+        i, j = rank // GC, rank % GC
+        s = _plan(RA, i)[2]
+        g.sync.dma_start(_slot(T, OWN_X), T.x[:]).then_inc(T.sem.ldx, 16)
+        g.scalar.dma_start(T.a0[:], T.a[:]).then_inc(T.sem.lda, 16)
+
+        off = topo.mask(core, comb[((i + 1) % GR, j)])
+        on_only = topo.mask(core, comb[(i, j)]) & ~off
+        g.wait_ge(T.sem.ldx, 16)
+        n = send(comb[((i + 1) % GR, j)], _slot(T, i), _slot(T, OWN_X), xa[i], off)
+        n += send(comb[(i, j)], _slot(T, i), _slot(T, OWN_X), xa[i], on_only)
+        for d in range(2, GR):
+            n += send(comb[((i + d) % GR, j)], _slot(T, i), _slot(T, OWN_X), xa[i], off)
+
+        coef = {OWN_X: CB[j][j] * RA[i][i], PAR_X: CB[j][1 - j] * RA[i][i], OWN_W: CB[j][j] * s, CROSS_W: CB[j][1 - j] * s}
+        vals = sorted(set(coef.values()))
+        tile = lambda t, q: t[:, q * M:(q + 1) * M]
+        for q, c in enumerate(vals):
+            g.vector.memset(tile(T.cst, q), float(c)).then_inc(T.sem.fill, 1)
+        g.vector.wait_ge(T.sem.fill, len(vals))
+        g.vector.wait_ge(T.sem.lda, 16)
+        for q, c in enumerate(vals):
+            g.vector.tensor_tensor(tile(T.asc, q), T.a0[:], tile(T.cst, q), AluOpType.mult).then_inc(T.sem.ascd, 1)
+
+        nc = _count(topo.mask(comb[(i, 1 - j)], core))
+        no = _count(topo.mask(comb[(i, j)], core) & ~topo.mask(comb[(i, j)], rank_at(i, 1 - j)))
+        g.tensor.wait_ge(T.sem.ascd, len(vals))
+        waits = [(OWN_X, T.sem.ldx, 16), (PAR_X, T.sem.xpar, nc), (OWN_W, T.sem.vown, no), (CROSS_W, T.sem.vcross, nc)]
+        for q, (piece, sem, cnt) in enumerate(waits):
+            g.tensor.wait_ge(sem, cnt)
+            mmi = g.tensor.matmul(T.pa[:], tile(T.asc, vals.index(coef[piece])), _slot(T, piece), q == 0, q == 3)
+        mmi.then_inc(T.sem.mm, 1)
+        g.vector.wait_ge(T.sem.mm, 1)
+        g.vector.tensor_copy(T.out[:], T.pa[:]).then_inc(T.sem.cp, 1)
+        g.sync.wait_ge(T.sem.cp, 1)
+        g.sync.dma_start(T.y[:], T.out[:]).then_inc(T.sem.st, 16)
+        g.sync.wait_ge(T.sem.st, 16)
+        g.wait_ge(T.sem.sent, n)
+        return
+
+    mine = [il for il in comb if comb[il] == core]
+    if not mine:
+        return
+    i, l = mine[0]
+    R, P = rank_at(i, l), rank_at(i, 1 - l)
+    order, steps, s = _plan(RA, i)
+    cross = topo.mask(core, P)
+    on_only = topo.mask(core, R) & ~cross
+    n_plane = {k: _count(topo.mask(rank_at(k, l), core)) for k in order}
+    n_own = _count(topo.mask(R, core) & ~topo.mask(R, comb[((i + 1) % GR, l)]))
+
+    g.wait_ge(xa[i], n_own)
+    n = send(P, _slot(T, PAR_X), _slot(T, i), T.sem.xpar, cross)
+
+    v = g.vector
+    facs = sorted(set(f for op, f in steps if op == "scale"))
+    for q, f in enumerate(facs):
+        v.memset(T.rs[:, q * W:(q + 1) * W], float(f)).then_inc(T.sem.fill, 1)
+    if facs:
+        v.wait_ge(T.sem.fill, len(facs))
+    banks = [T.pa, T.pb]
+    v.wait_ge(xa[order[0]], n_plane[order[0]])
+    cur = _slot(T, order[0])
+    for done, (op, arg) in enumerate(steps):
+        if done:
+            v.wait_ge(T.sem.vs, done)
+        out = T.out[:] if done == len(steps) - 1 else banks[done % 2][:]
+        if op == "scale":
+            q = facs.index(arg)
+            v.tensor_tensor(out, cur, T.rs[:, q * W:(q + 1) * W], AluOpType.mult).then_inc(T.sem.vs, 1)
+        else:
+            v.wait_ge(xa[arg], n_plane[arg])
+            v.tensor_tensor(out, cur, _slot(T, arg), AluOpType.add if op == "add" else AluOpType.subtract
+                            ).then_inc(T.sem.vs, 1)
+        cur = out
+
+    g.wait_ge(T.sem.vs, len(steps))
+    rp, pp = topo.addr(P, core)
+    rr, pr = topo.addr(R, core)
+    g.remote_dma_fused([
+        RemoteDMATransfer(dst_ids=[DstId(rid=rp, pnc=pp)], dma_engine_mask=cross, remote_sem=T.sem.vcross,
+                          src=T.out[:], dst=_slot(T, CROSS_W)),
+        RemoteDMATransfer(dst_ids=[DstId(rid=rr, pnc=pr)], dma_engine_mask=on_only, remote_sem=T.sem.vown,
+                          src=T.out[:], dst=_slot(T, OWN_W)),
+    ], local_sem=T.sem.sent)
+    n += _count(cross) + _count(on_only)
+    g.wait_ge(T.sem.sent, n)

@@ -3,6 +3,7 @@ from concourse.mybir import AluOpType
 
 WORLD = 256
 GR, GC, W, M = 4, 2, 512, 128
+H = W // 2
 
 SCRATCH = {
     "land": ("sbuf", [128, 4 * W], "bfloat16"),
@@ -14,8 +15,8 @@ SCRATCH = {
     "pa": ("psum", [128, W], "float32"),
     "pb": ("psum", [128, W], "float32"),
 }
-SEMAPHORES = ["ldx", "lda", "fill", "ascd", "mm", "cp", "st", "sent", "vs",
-              "xa0", "xa1", "xa2", "xa3", "xpar", "vown", "vcross"]
+SEMAPHORES = ["ldx", "lda", "fill", "ascd", "mm0", "mm1", "cp0", "cp1", "st0", "st1", "sent", "vs", "vf0", "vf1",
+              "xa0", "xa1", "xa2", "xa3", "xl0", "xl1", "xpar", "vown0", "vown1", "vcross0", "vcross1"]
 OWN_X, PAR_X, OWN_W, CROSS_W = 0, 1, 2, 3
 
 
@@ -23,9 +24,28 @@ def _count(mask):
     return bin(mask).count("1")
 
 
-def _plan(RA, i):
-    order = [(i - d) % GR for d in range(1, GR)]
-    steps, s = [], RA[i][order[0]]
+def _perms(items):
+    if len(items) <= 1:
+        return [list(items)]
+    return [[items[q]] + p for q in range(len(items)) for p in _perms(items[:q] + items[q + 1:])]
+
+
+def _rounds(RA):
+    ders = [p for p in _perms(list(range(GR))) if all(p[k] != k for k in range(GR))]
+    best = None
+    for r in [[p1, p2, p3] for p1 in ders for p2 in ders for p3 in ders]:
+        if any(len(set(p[k] for p in r)) != GR - 1 for k in range(GR)):
+            continue
+        cost = sum(abs(RA[i][r[-2].index(i)]) != abs(RA[i][r[-1].index(i)]) for i in range(GR))
+        if best is None or cost < best[0]:
+            best = (cost, r)
+    return best[1]
+
+
+def _plan(RA, rounds, i):
+    order = [p.index(i) for p in rounds]
+    f0 = abs(RA[i][order[0]]) / abs(RA[i][order[1]])
+    steps, s = [("init", f0)], RA[i][order[0]] / f0
     for k in order[1:]:
         c = RA[i][k]
         if abs(c) != abs(s):
@@ -39,18 +59,30 @@ def _plan(RA, i):
 def _combiner(topo, R, P):
     c = [c for c in range(WORLD) if c != R and topo.host(c) == topo.host(R) and topo.chip(c) == topo.chip(R)
          and topo.may_write(c, P)]
-    return sorted(c, key=lambda c: (topo.die(c) != topo.die(R), c))[0]
+    return sorted(c, key=lambda c: (topo.die(c) == topo.die(R), c))[0]
 
 
 def _slot(T, q):
     return T.land[:, q * W:(q + 1) * W]
 
 
+def _half(T, q, h):
+    return T.land[:, q * W + h * H:q * W + (h + 1) * H]
+
+
 def rank_program(g, core, T, topo):
     RA, CB = T.tables["RA"], T.tables["CB"]
     rank_at = lambda i, l: T.cores[i * GC + l]
     comb = {(i, l): _combiner(topo, rank_at(i, l), rank_at(i, 1 - l)) for i in range(GR) for l in range(GC)}
+    rank = T.rank_of(core)
+    mine = [il for il in comb if comb[il] == core]
+    if rank is None and not mine:
+        return
     xa = [T.sem["xa%d" % k] for k in range(GR)]
+    sem2 = lambda name: [T.sem[name + "0"], T.sem[name + "1"]]
+    xl, vown, vcross = sem2("xl"), sem2("vown"), sem2("vcross")
+    rounds = _rounds(RA)
+    v = g.vector
 
     def send(dst, out_ap, in_ap, sem, mask):
         rid, pid = topo.addr(dst, core)
@@ -58,63 +90,77 @@ def rank_program(g, core, T, topo):
                      dma_engine_mask=mask)
         return _count(mask)
 
-    rank = T.rank_of(core)
+    def transfer(dst, out_ap, in_ap, sem, mask):
+        rid, pid = topo.addr(dst, core)
+        return RemoteDMATransfer(dst_ids=[DstId(rid=rid, pnc=pid)], dma_engine_mask=mask, remote_sem=sem,
+                                 src=in_ap, dst=out_ap)
+
     if rank is not None:
         i, j = rank // GC, rank % GC
-        s = _plan(RA, i)[2]
+        s = _plan(RA, rounds, i)[2]
         g.sync.dma_start(_slot(T, OWN_X), T.x[:]).then_inc(T.sem.ldx, 16)
         g.scalar.dma_start(T.a0[:], T.a[:]).then_inc(T.sem.lda, 16)
 
-        off = topo.mask(core, comb[((i + 1) % GR, j)])
+        peers = [comb[(p[i], j)] for p in rounds]
+        off = topo.mask(core, peers[0])
         on_only = topo.mask(core, comb[(i, j)]) & ~off
         g.wait_ge(T.sem.ldx, 16)
-        n = send(comb[((i + 1) % GR, j)], _slot(T, i), _slot(T, OWN_X), xa[i], off)
+        ids = [topo.addr(p, core) for p in peers[:-1]]
+        g.remote_dma_fused([RemoteDMATransfer(dst_ids=[DstId(rid=r, pnc=p) for r, p in ids], dma_engine_mask=off,
+                                              remote_sem=xa[i], srcs=[_slot(T, OWN_X)], dsts=[_slot(T, i) for p in ids])],
+                           local_sem=T.sem.sent)
+        n = _count(off)
         n += send(comb[(i, j)], _slot(T, i), _slot(T, OWN_X), xa[i], on_only)
-        for d in range(2, GR):
-            n += send(comb[((i + d) % GR, j)], _slot(T, i), _slot(T, OWN_X), xa[i], off)
+        for h in range(2):
+            n += send(peers[-1], _half(T, i, h), _half(T, OWN_X, h), xl[h], off)
 
         coef = {OWN_X: CB[j][j] * RA[i][i], PAR_X: CB[j][1 - j] * RA[i][i], OWN_W: CB[j][j] * s, CROSS_W: CB[j][1 - j] * s}
         vals = sorted(set(coef.values()))
         tile = lambda t, q: t[:, q * M:(q + 1) * M]
         for q, c in enumerate(vals):
-            g.vector.memset(tile(T.cst, q), float(c)).then_inc(T.sem.fill, 1)
-        g.vector.wait_ge(T.sem.fill, len(vals))
-        g.vector.wait_ge(T.sem.lda, 16)
+            v.memset(tile(T.cst, q), float(c)).then_inc(T.sem.fill, 1)
+        v.wait_ge(T.sem.fill, len(vals))
+        v.wait_ge(T.sem.lda, 16)
         for q, c in enumerate(vals):
-            g.vector.tensor_tensor(tile(T.asc, q), T.a0[:], tile(T.cst, q), AluOpType.mult).then_inc(T.sem.ascd, 1)
+            v.tensor_tensor(tile(T.asc, q), T.a0[:], tile(T.cst, q), AluOpType.mult).then_inc(T.sem.ascd, 1)
 
         nc = _count(topo.mask(comb[(i, 1 - j)], core))
         no = _count(topo.mask(comb[(i, j)], core) & ~topo.mask(comb[(i, j)], rank_at(i, 1 - j)))
+        banks, mm, cp, st, queues = [T.pa, T.pb], sem2("mm"), sem2("cp"), sem2("st"), [g.sync, g.scalar]
+        mul = lambda piece, h, first, last: g.tensor.matmul(banks[h][:, 0:H], tile(T.asc, vals.index(coef[piece])),
+                                                            _half(T, piece, h), first, last)
         g.tensor.wait_ge(T.sem.ascd, len(vals))
-        waits = [(OWN_X, T.sem.ldx, 16), (PAR_X, T.sem.xpar, nc), (OWN_W, T.sem.vown, no), (CROSS_W, T.sem.vcross, nc)]
-        for q, (piece, sem, cnt) in enumerate(waits):
-            g.tensor.wait_ge(sem, cnt)
-            mmi = g.tensor.matmul(T.pa[:], tile(T.asc, vals.index(coef[piece])), _slot(T, piece), q == 0, q == 3)
-        mmi.then_inc(T.sem.mm, 1)
-        g.vector.wait_ge(T.sem.mm, 1)
-        g.vector.tensor_copy(T.out[:], T.pa[:]).then_inc(T.sem.cp, 1)
-        g.sync.wait_ge(T.sem.cp, 1)
-        g.sync.dma_start(T.y[:], T.out[:]).then_inc(T.sem.st, 16)
-        g.sync.wait_ge(T.sem.st, 16)
+        g.tensor.wait_ge(T.sem.ldx, 16)
+        for h in range(2):
+            mul(OWN_X, h, True, False)
+        g.tensor.wait_ge(T.sem.xpar, nc)
+        for h in range(2):
+            mul(PAR_X, h, False, False)
+        for h in range(2):
+            g.tensor.wait_ge(vown[h], no)
+            mul(OWN_W, h, False, False)
+            g.tensor.wait_ge(vcross[h], nc)
+            mul(CROSS_W, h, False, True).then_inc(mm[h], 1)
+            v.wait_ge(mm[h], 1)
+            v.tensor_copy(T.out[:, h * H:(h + 1) * H], banks[h][:, 0:H]).then_inc(cp[h], 1)
+            queues[h].wait_ge(cp[h], 1)
+            queues[h].dma_start(T.y[:, h * H:(h + 1) * H], T.out[:, h * H:(h + 1) * H]).then_inc(st[h], 16)
+            queues[h].wait_ge(st[h], 16)
         g.wait_ge(T.sem.sent, n)
         return
 
-    mine = [il for il in comb if comb[il] == core]
-    if not mine:
-        return
     i, l = mine[0]
     R, P = rank_at(i, l), rank_at(i, 1 - l)
-    order, steps, s = _plan(RA, i)
+    order, steps, s = _plan(RA, rounds, i)
     cross = topo.mask(core, P)
     on_only = topo.mask(core, R) & ~cross
     n_plane = {k: _count(topo.mask(rank_at(k, l), core)) for k in order}
-    n_own = _count(topo.mask(R, core) & ~topo.mask(R, comb[((i + 1) % GR, l)]))
+    n_own = _count(topo.mask(R, core) & ~topo.mask(R, comb[(rounds[0][i], l)]))
 
     g.wait_ge(xa[i], n_own)
     n = send(P, _slot(T, PAR_X), _slot(T, i), T.sem.xpar, cross)
 
-    v = g.vector
-    facs = sorted(set(f for op, f in steps if op == "scale"))
+    facs = sorted(set(f for op, f in steps if op in ("init", "scale") and f != 1))
     for q, f in enumerate(facs):
         v.memset(T.rs[:, q * W:(q + 1) * W], float(f)).then_inc(T.sem.fill, 1)
     if facs:
@@ -122,27 +168,32 @@ def rank_program(g, core, T, topo):
     banks = [T.pa, T.pb]
     v.wait_ge(xa[order[0]], n_plane[order[0]])
     cur = _slot(T, order[0])
-    for done, (op, arg) in enumerate(steps):
+    for done, (op, arg) in enumerate(steps[:-1]):
         if done:
             v.wait_ge(T.sem.vs, done)
-        out = T.out[:] if done == len(steps) - 1 else banks[done % 2][:]
-        if op == "scale":
-            q = facs.index(arg)
-            v.tensor_tensor(out, cur, T.rs[:, q * W:(q + 1) * W], AluOpType.mult).then_inc(T.sem.vs, 1)
+        out = banks[done % 2][:]
+        if op in ("init", "scale"):
+            if arg == 1:
+                v.tensor_copy(out, cur).then_inc(T.sem.vs, 1)
+            else:
+                q = facs.index(arg)
+                v.tensor_tensor(out, cur, T.rs[:, q * W:(q + 1) * W], AluOpType.mult).then_inc(T.sem.vs, 1)
         else:
             v.wait_ge(xa[arg], n_plane[arg])
             v.tensor_tensor(out, cur, _slot(T, arg), AluOpType.add if op == "add" else AluOpType.subtract
                             ).then_inc(T.sem.vs, 1)
         cur = out
-
-    g.wait_ge(T.sem.vs, len(steps))
-    rp, pp = topo.addr(P, core)
-    rr, pr = topo.addr(R, core)
-    g.remote_dma_fused([
-        RemoteDMATransfer(dst_ids=[DstId(rid=rp, pnc=pp)], dma_engine_mask=cross, remote_sem=T.sem.vcross,
-                          src=T.out[:], dst=_slot(T, CROSS_W)),
-        RemoteDMATransfer(dst_ids=[DstId(rid=rr, pnc=pr)], dma_engine_mask=on_only, remote_sem=T.sem.vown,
-                          src=T.out[:], dst=_slot(T, OWN_W)),
-    ], local_sem=T.sem.sent)
-    n += _count(cross) + _count(on_only)
+    v.wait_ge(T.sem.vs, len(steps) - 1)
+    acc = banks[(len(steps) - 2) % 2]
+    op, last = steps[-1]
+    vf = sem2("vf")
+    for h in range(2):
+        v.wait_ge(xl[h], n_plane[last])
+        v.tensor_tensor(T.out[:, h * H:(h + 1) * H], acc[:, h * H:(h + 1) * H], _half(T, last, h),
+                        AluOpType.add if op == "add" else AluOpType.subtract).then_inc(vf[h], 1)
+        g.wait_ge(vf[h], 1)
+        g.remote_dma_fused([transfer(P, _half(T, CROSS_W, h), T.out[:, h * H:(h + 1) * H], vcross[h], cross),
+                            transfer(R, _half(T, OWN_W, h), T.out[:, h * H:(h + 1) * H], vown[h], on_only)],
+                           local_sem=T.sem.sent)
+        n += _count(cross) + _count(on_only)
     g.wait_ge(T.sem.sent, n)

@@ -6,18 +6,18 @@ GR, GC, W, M = 4, 2, 512, 128
 H = W // 2
 
 SCRATCH = {
-    "land": ("sbuf", [128, 4 * W], "bfloat16"),
+    "land": ("sbuf", [128, 5 * W], "bfloat16"),
     "out": ("sbuf", [128, W], "bfloat16"),
     "a0": ("sbuf", [128, M], "bfloat16"),
     "cst": ("sbuf", [128, 4 * M], "bfloat16"),
     "asc": ("sbuf", [128, 4 * M], "bfloat16"),
-    "rs": ("sbuf", [128, 2 * W], "float32"),
+    "rs": ("sbuf", [128, 2 * H], "float32"),
     "pa": ("psum", [128, W], "float32"),
     "pb": ("psum", [128, W], "float32"),
 }
-SEMAPHORES = ["ldx", "lda", "fill", "ascd", "mm0", "mm1", "cp0", "cp1", "st0", "st1", "sent", "vs", "vf0", "vf1",
-              "xa0", "xa1", "xa2", "xa3", "xl0", "xl1", "xpar", "vown0", "vown1", "vcross0", "vcross1"]
-OWN_X, PAR_X, OWN_W, CROSS_W = 0, 1, 2, 3
+SEMAPHORES = ["ldx", "lda", "fill", "ascd", "mm0", "mm1", "cp0", "cp1", "st0", "st1", "sent", "vs", "vf",
+              "xa0", "xa1", "xa2", "xa3", "xr", "xp0", "xp1", "vown0", "vown1", "vcross0", "vcross1"]
+RAW_P, RAW_X, OWN_W, CROSS_W, OWN_X = 0, 1, 2, 3, 4
 
 
 def _count(mask):
@@ -36,14 +36,14 @@ def _rounds(RA):
     for r in [[p1, p2, p3] for p1 in ders for p2 in ders for p3 in ders]:
         if any(len(set(p[k] for p in r)) != GR - 1 for k in range(GR)):
             continue
-        cost = sum(abs(RA[i][r[-2].index(i)]) != abs(RA[i][r[-1].index(i)]) for i in range(GR))
+        cost = sum(abs(RA[i][r[0].index(i)]) != abs(RA[i][r[1].index(i)]) for i in range(GR))
         if best is None or cost < best[0]:
             best = (cost, r)
     return best[1]
 
 
 def _plan(RA, rounds, i):
-    order = [p.index(i) for p in rounds]
+    order = [i] + [p.index(i) for p in rounds[:-1]]
     f0 = abs(RA[i][order[0]]) / abs(RA[i][order[1]])
     steps, s = [("init", f0)], RA[i][order[0]] / f0
     for k in order[1:]:
@@ -56,10 +56,10 @@ def _plan(RA, rounds, i):
     return order, steps, s
 
 
-def _combiner(topo, R, P):
+def _combiners(topo, R, targets):
     c = [c for c in range(WORLD) if c != R and topo.host(c) == topo.host(R) and topo.chip(c) == topo.chip(R)
-         and topo.may_write(c, P)]
-    return sorted(c, key=lambda c: (topo.die(c) == topo.die(R), c))[0]
+         and all(topo.may_write(c, t) for t in targets)]
+    return sorted(c, key=lambda c: (topo.die(c) == topo.die(R), c))[:2]
 
 
 def _slot(T, q):
@@ -73,14 +73,15 @@ def _half(T, q, h):
 def rank_program(g, core, T, topo):
     RA, CB = T.tables["RA"], T.tables["CB"]
     rank_at = lambda i, l: T.cores[i * GC + l]
-    comb = {(i, l): _combiner(topo, rank_at(i, l), rank_at(i, 1 - l)) for i in range(GR) for l in range(GC)}
+    comb = {(i, l): _combiners(topo, rank_at(i, l), [rank_at(k, 1 - l) for k in range(GR)])
+            for i in range(GR) for l in range(GC)}
     rank = T.rank_of(core)
-    mine = [il for il in comb if comb[il] == core]
+    mine = [(il[0], il[1], h) for il in comb for h in range(2) if comb[il][h] == core]
     if rank is None and not mine:
         return
     xa = [T.sem["xa%d" % k] for k in range(GR)]
     sem2 = lambda name: [T.sem[name + "0"], T.sem[name + "1"]]
-    xl, vown, vcross = sem2("xl"), sem2("vown"), sem2("vcross")
+    xp, vown, vcross = sem2("xp"), sem2("vown"), sem2("vcross")
     rounds = _rounds(RA)
     v = g.vector
 
@@ -101,20 +102,28 @@ def rank_program(g, core, T, topo):
         g.sync.dma_start(_slot(T, OWN_X), T.x[:]).then_inc(T.sem.ldx, 16)
         g.scalar.dma_start(T.a0[:], T.a[:]).then_inc(T.sem.lda, 16)
 
-        peers = [comb[(p[i], j)] for p in rounds]
-        off = topo.mask(core, peers[0])
-        on_only = topo.mask(core, comb[(i, j)]) & ~off
+        k3 = rounds[-1].index(i)
+        third = rank_at(rounds[-1][i], j)
         g.wait_ge(T.sem.ldx, 16)
-        ids = [topo.addr(p, core) for p in peers[:-1]]
-        g.remote_dma_fused([RemoteDMATransfer(dst_ids=[DstId(rid=r, pnc=p) for r, p in ids], dma_engine_mask=off,
-                                              remote_sem=xa[i], srcs=[_slot(T, OWN_X)], dsts=[_slot(T, i) for p in ids])],
-                           local_sem=T.sem.sent)
-        n = _count(off)
-        n += send(comb[(i, j)], _slot(T, i), _slot(T, OWN_X), xa[i], on_only)
+        n = 0
         for h in range(2):
-            n += send(peers[-1], _half(T, i, h), _half(T, OWN_X, h), xl[h], off)
+            peers = [comb[(p[i], j)][h] for p in rounds[:-1]]
+            own = comb[(i, j)][h]
+            off = topo.mask(core, peers[0])
+            on_only = topo.mask(core, own) & ~off
+            ids = [topo.addr(p, core) for p in peers]
+            plane = RemoteDMATransfer(dst_ids=[DstId(rid=r, pnc=p) for r, p in ids], dma_engine_mask=off, remote_sem=xa[i],
+                                      srcs=[_half(T, OWN_X, h)], dsts=[_half(T, i, h) for p in ids])
+            hand = transfer(own, _half(T, i, h), _half(T, OWN_X, h), xa[i], on_only)
+            if h == 0:
+                g.remote_dma_fused([plane], local_sem=T.sem.sent)
+                g.remote_dma_fused([hand], local_sem=T.sem.sent)
+            else:
+                g.remote_dma_fused([plane, hand], local_sem=T.sem.sent)
+            n += _count(off) + _count(on_only)
+        n += send(third, _slot(T, RAW_P), _slot(T, OWN_X), T.sem.xr, topo.mask(core, third))
 
-        coef = {OWN_X: CB[j][j] * RA[i][i], PAR_X: CB[j][1 - j] * RA[i][i], OWN_W: CB[j][j] * s, CROSS_W: CB[j][1 - j] * s}
+        coef = {RAW_P: CB[j][j] * RA[i][k3], RAW_X: CB[j][1 - j] * RA[i][k3], OWN_W: CB[j][j] * s, CROSS_W: CB[j][1 - j] * s}
         vals = sorted(set(coef.values()))
         tile = lambda t, q: t[:, q * M:(q + 1) * M]
         for q, c in enumerate(vals):
@@ -124,23 +133,29 @@ def rank_program(g, core, T, topo):
         for q, c in enumerate(vals):
             v.tensor_tensor(tile(T.asc, q), T.a0[:], tile(T.cst, q), AluOpType.mult).then_inc(T.sem.ascd, 1)
 
-        nc = _count(topo.mask(comb[(i, 1 - j)], core))
-        no = _count(topo.mask(comb[(i, j)], core) & ~topo.mask(comb[(i, j)], rank_at(i, 1 - j)))
+        n_rx = [_count(topo.mask(comb[(k3, 1 - j)][h], core)) for h in range(2)]
+        n_rp = _count(topo.mask(rank_at(k3, j), core))
+        nc = [_count(topo.mask(comb[(i, 1 - j)][h], core)) for h in range(2)]
+        no = [_count(topo.mask(comb[(i, j)][h], core) & ~topo.mask(comb[(i, j)][h], rank_at(i, 1 - j))) for h in range(2)]
         banks, mm, cp, st, queues = [T.pa, T.pb], sem2("mm"), sem2("cp"), sem2("st"), [g.sync, g.scalar]
         mul = lambda piece, h, first, last: g.tensor.matmul(banks[h][:, 0:H], tile(T.asc, vals.index(coef[piece])),
                                                             _half(T, piece, h), first, last)
         g.tensor.wait_ge(T.sem.ascd, len(vals))
-        g.tensor.wait_ge(T.sem.ldx, 16)
         for h in range(2):
-            mul(OWN_X, h, True, False)
-        g.tensor.wait_ge(T.sem.xpar, nc)
+            g.tensor.wait_ge(xp[h], n_rx[h])
+            mul(RAW_X, h, True, False)
+        g.tensor.wait_ge(vown[0], no[0])
+        mul(OWN_W, 0, False, False)
+        g.tensor.wait_ge(vcross[0], nc[0])
+        mul(CROSS_W, 0, False, False)
+        g.tensor.wait_ge(T.sem.xr, n_rp)
+        mul(RAW_P, 0, False, True).then_inc(mm[0], 1)
+        mul(RAW_P, 1, False, False)
+        g.tensor.wait_ge(vown[1], no[1])
+        mul(OWN_W, 1, False, False)
+        g.tensor.wait_ge(vcross[1], nc[1])
+        mul(CROSS_W, 1, False, True).then_inc(mm[1], 1)
         for h in range(2):
-            mul(PAR_X, h, False, False)
-        for h in range(2):
-            g.tensor.wait_ge(vown[h], no)
-            mul(OWN_W, h, False, False)
-            g.tensor.wait_ge(vcross[h], nc)
-            mul(CROSS_W, h, False, True).then_inc(mm[h], 1)
             v.wait_ge(mm[h], 1)
             v.tensor_copy(T.out[:, h * H:(h + 1) * H], banks[h][:, 0:H]).then_inc(cp[h], 1)
             queues[h].wait_ge(cp[h], 1)
@@ -149,51 +164,49 @@ def rank_program(g, core, T, topo):
         g.wait_ge(T.sem.sent, n)
         return
 
-    i, l = mine[0]
+    i, l, h = mine[0]
     R, P = rank_at(i, l), rank_at(i, 1 - l)
     order, steps, s = _plan(RA, rounds, i)
     cross = topo.mask(core, P)
     on_only = topo.mask(core, R) & ~cross
-    n_plane = {k: _count(topo.mask(rank_at(k, l), core)) for k in order}
-    n_own = _count(topo.mask(R, core) & ~topo.mask(R, comb[(rounds[0][i], l)]))
+    n_in = {k: _count(topo.mask(rank_at(k, l), core)) for k in order[1:]}
+    n_in[i] = _count(topo.mask(R, core) & ~topo.mask(R, comb[(rounds[0][i], l)][h]))
 
-    g.wait_ge(xa[i], n_own)
-    n = send(P, _slot(T, PAR_X), _slot(T, i), T.sem.xpar, cross)
+    Q = rank_at(rounds[-1][i], 1 - l)
+    g.wait_ge(xa[i], n_in[i])
+    n = send(Q, _half(T, RAW_X, h), _half(T, i, h), xp[h], topo.mask(core, Q))
 
     facs = sorted(set(f for op, f in steps if op in ("init", "scale") and f != 1))
     for q, f in enumerate(facs):
-        v.memset(T.rs[:, q * W:(q + 1) * W], float(f)).then_inc(T.sem.fill, 1)
+        v.memset(T.rs[:, q * H:(q + 1) * H], float(f)).then_inc(T.sem.fill, 1)
     if facs:
         v.wait_ge(T.sem.fill, len(facs))
     banks = [T.pa, T.pb]
-    v.wait_ge(xa[order[0]], n_plane[order[0]])
-    cur = _slot(T, order[0])
+    v.wait_ge(xa[order[0]], n_in[order[0]])
+    cur = _half(T, order[0], h)
     for done, (op, arg) in enumerate(steps[:-1]):
         if done:
             v.wait_ge(T.sem.vs, done)
-        out = banks[done % 2][:]
+        out = banks[done % 2][:, 0:H]
         if op in ("init", "scale"):
             if arg == 1:
                 v.tensor_copy(out, cur).then_inc(T.sem.vs, 1)
             else:
                 q = facs.index(arg)
-                v.tensor_tensor(out, cur, T.rs[:, q * W:(q + 1) * W], AluOpType.mult).then_inc(T.sem.vs, 1)
+                v.tensor_tensor(out, cur, T.rs[:, q * H:(q + 1) * H], AluOpType.mult).then_inc(T.sem.vs, 1)
         else:
-            v.wait_ge(xa[arg], n_plane[arg])
-            v.tensor_tensor(out, cur, _slot(T, arg), AluOpType.add if op == "add" else AluOpType.subtract
+            v.wait_ge(xa[arg], n_in[arg])
+            v.tensor_tensor(out, cur, _half(T, arg, h), AluOpType.add if op == "add" else AluOpType.subtract
                             ).then_inc(T.sem.vs, 1)
         cur = out
     v.wait_ge(T.sem.vs, len(steps) - 1)
-    acc = banks[(len(steps) - 2) % 2]
     op, last = steps[-1]
-    vf = sem2("vf")
-    for h in range(2):
-        v.wait_ge(xl[h], n_plane[last])
-        v.tensor_tensor(T.out[:, h * H:(h + 1) * H], acc[:, h * H:(h + 1) * H], _half(T, last, h),
-                        AluOpType.add if op == "add" else AluOpType.subtract).then_inc(vf[h], 1)
-        g.wait_ge(vf[h], 1)
-        g.remote_dma_fused([transfer(P, _half(T, CROSS_W, h), T.out[:, h * H:(h + 1) * H], vcross[h], cross),
-                            transfer(R, _half(T, OWN_W, h), T.out[:, h * H:(h + 1) * H], vown[h], on_only)],
-                           local_sem=T.sem.sent)
-        n += _count(cross) + _count(on_only)
+    v.wait_ge(xa[last], n_in[last])
+    v.tensor_tensor(T.out[:, 0:H], cur, _half(T, last, h),
+                    AluOpType.add if op == "add" else AluOpType.subtract).then_inc(T.sem.vf, 1)
+    g.wait_ge(T.sem.vf, 1)
+    g.remote_dma_fused([transfer(P, _half(T, CROSS_W, h), T.out[:, 0:H], vcross[h], cross),
+                        transfer(R, _half(T, OWN_W, h), T.out[:, 0:H], vown[h], on_only)],
+                       local_sem=T.sem.sent)
+    n += _count(cross) + _count(on_only)
     g.wait_ge(T.sem.sent, n)

from concourse.bass import DstId, RemoteDMATransfer
from concourse.mybir import AluOpType

WORLD = 256
GR, GC, W, M = 4, 2, 512, 128
H = W // 2

SCRATCH = {
    "land": ("sbuf", [128, 5 * W], "bfloat16"),
    "out": ("sbuf", [128, W], "bfloat16"),
    "a0": ("sbuf", [128, M], "bfloat16"),
    "cst": ("sbuf", [128, 4 * M], "bfloat16"),
    "asc": ("sbuf", [128, 4 * M], "bfloat16"),
    "rs": ("sbuf", [128, 2 * H], "float32"),
    "pa": ("psum", [128, W], "float32"),
    "pb": ("psum", [128, W], "float32"),
}
SEMAPHORES = ["ldx", "lda", "fill", "ascd", "mm0", "mm1", "cp0", "cp1", "st0", "st1", "sent", "vs", "vf",
              "xa0", "xa1", "xa2", "xa3", "xr", "xp0", "xp1", "vown0", "vown1", "vcross0", "vcross1"]
RAW_P, RAW_X, OWN_W, CROSS_W, OWN_X = 0, 1, 2, 3, 4


def _count(mask):
    return bin(mask).count("1")


def _perms(items):
    if len(items) <= 1:
        return [list(items)]
    return [[items[q]] + p for q in range(len(items)) for p in _perms(items[:q] + items[q + 1:])]


def _rounds(RA):
    ders = [p for p in _perms(list(range(GR))) if all(p[k] != k for k in range(GR))]
    best = None
    for r in [[p1, p2, p3] for p1 in ders for p2 in ders for p3 in ders]:
        if any(len(set(p[k] for p in r)) != GR - 1 for k in range(GR)):
            continue
        cost = sum(abs(RA[i][r[0].index(i)]) != abs(RA[i][r[1].index(i)]) for i in range(GR))
        if best is None or cost < best[0]:
            best = (cost, r)
    return best[1]


def _plan(RA, rounds, i):
    order = [i] + [p.index(i) for p in rounds[:-1]]
    f0 = abs(RA[i][order[0]]) / abs(RA[i][order[1]])
    steps, s = [("init", f0)], RA[i][order[0]] / f0
    for k in order[1:]:
        c = RA[i][k]
        if abs(c) != abs(s):
            f = abs(s) / abs(c)
            steps.append(("scale", f))
            s = s / f
        steps.append(("add" if c == s else "sub", k))
    return order, steps, s


def _combiners(topo, R, targets):
    c = [c for c in range(WORLD) if c != R and topo.host(c) == topo.host(R) and topo.chip(c) == topo.chip(R)
         and all(topo.may_write(c, t) for t in targets)]
    return sorted(c, key=lambda c: (topo.die(c) == topo.die(R), c))[:2]


def _slot(T, q):
    return T.land[:, q * W:(q + 1) * W]


def _half(T, q, h):
    return T.land[:, q * W + h * H:q * W + (h + 1) * H]


def rank_program(g, core, T, topo):
    RA, CB = T.tables["RA"], T.tables["CB"]
    rank_at = lambda i, l: T.cores[i * GC + l]
    comb = {(i, l): _combiners(topo, rank_at(i, l), [rank_at(k, 1 - l) for k in range(GR)])
            for i in range(GR) for l in range(GC)}
    rank = T.rank_of(core)
    mine = [(il[0], il[1], h) for il in comb for h in range(2) if comb[il][h] == core]
    if rank is None and not mine:
        return
    xa = [T.sem["xa%d" % k] for k in range(GR)]
    sem2 = lambda name: [T.sem[name + "0"], T.sem[name + "1"]]
    xp, vown, vcross = sem2("xp"), sem2("vown"), sem2("vcross")
    rounds = _rounds(RA)
    v = g.vector

    def send(dst, out_ap, in_ap, sem, mask):
        rid, pid = topo.addr(dst, core)
        g.remote_dma(out_ap=out_ap, in_ap=in_ap, remote_sem=sem, local_sem=T.sem.sent, pid=pid, routing_id=rid,
                     dma_engine_mask=mask)
        return _count(mask)

    def transfer(dst, out_ap, in_ap, sem, mask):
        rid, pid = topo.addr(dst, core)
        return RemoteDMATransfer(dst_ids=[DstId(rid=rid, pnc=pid)], dma_engine_mask=mask, remote_sem=sem,
                                 src=in_ap, dst=out_ap)

    if rank is not None:
        i, j = rank // GC, rank % GC
        s = _plan(RA, rounds, i)[2]
        g.sync.dma_start(_slot(T, OWN_X), T.x[:]).then_inc(T.sem.ldx, 16)
        g.scalar.dma_start(T.a0[:], T.a[:]).then_inc(T.sem.lda, 16)

        k3 = rounds[-1].index(i)
        third = rank_at(rounds[-1][i], j)
        g.wait_ge(T.sem.ldx, 16)
        n = 0
        for h in range(2):
            peers = [comb[(p[i], j)][h] for p in rounds[:-1]]
            own = comb[(i, j)][h]
            off = topo.mask(core, peers[0])
            on_only = topo.mask(core, own) & ~off
            ids = [topo.addr(p, core) for p in peers]
            plane = RemoteDMATransfer(dst_ids=[DstId(rid=r, pnc=p) for r, p in ids], dma_engine_mask=off, remote_sem=xa[i],
                                      srcs=[_half(T, OWN_X, h)], dsts=[_half(T, i, h) for p in ids])
            hand = transfer(own, _half(T, i, h), _half(T, OWN_X, h), xa[i], on_only)
            if h == 0:
                g.remote_dma_fused([plane], local_sem=T.sem.sent)
                g.remote_dma_fused([hand], local_sem=T.sem.sent)
            else:
                g.remote_dma_fused([plane, hand], local_sem=T.sem.sent)
            n += _count(off) + _count(on_only)
        n += send(third, _slot(T, RAW_P), _slot(T, OWN_X), T.sem.xr, topo.mask(core, third))

        coef = {RAW_P: CB[j][j] * RA[i][k3], RAW_X: CB[j][1 - j] * RA[i][k3], OWN_W: CB[j][j] * s, CROSS_W: CB[j][1 - j] * s}
        vals = sorted(set(coef.values()))
        tile = lambda t, q: t[:, q * M:(q + 1) * M]
        for q, c in enumerate(vals):
            v.memset(tile(T.cst, q), float(c)).then_inc(T.sem.fill, 1)
        v.wait_ge(T.sem.fill, len(vals))
        v.wait_ge(T.sem.lda, 16)
        for q, c in enumerate(vals):
            v.tensor_tensor(tile(T.asc, q), T.a0[:], tile(T.cst, q), AluOpType.mult).then_inc(T.sem.ascd, 1)

        n_rx = [_count(topo.mask(comb[(k3, 1 - j)][h], core)) for h in range(2)]
        n_rp = _count(topo.mask(rank_at(k3, j), core))
        nc = [_count(topo.mask(comb[(i, 1 - j)][h], core)) for h in range(2)]
        no = [_count(topo.mask(comb[(i, j)][h], core) & ~topo.mask(comb[(i, j)][h], rank_at(i, 1 - j))) for h in range(2)]
        banks, mm, cp, st, queues = [T.pa, T.pb], sem2("mm"), sem2("cp"), sem2("st"), [g.sync, g.scalar]
        mul = lambda piece, h, first, last: g.tensor.matmul(banks[h][:, 0:H], tile(T.asc, vals.index(coef[piece])),
                                                            _half(T, piece, h), first, last)
        g.tensor.wait_ge(T.sem.ascd, len(vals))
        for h in range(2):
            g.tensor.wait_ge(xp[h], n_rx[h])
            mul(RAW_X, h, True, False)
        g.tensor.wait_ge(vown[0], no[0])
        mul(OWN_W, 0, False, False)
        g.tensor.wait_ge(vcross[0], nc[0])
        mul(CROSS_W, 0, False, False)
        g.tensor.wait_ge(T.sem.xr, n_rp)
        mul(RAW_P, 0, False, True).then_inc(mm[0], 1)
        mul(RAW_P, 1, False, False)
        g.tensor.wait_ge(vown[1], no[1])
        mul(OWN_W, 1, False, False)
        g.tensor.wait_ge(vcross[1], nc[1])
        mul(CROSS_W, 1, False, True).then_inc(mm[1], 1)
        for h in range(2):
            v.wait_ge(mm[h], 1)
            v.tensor_copy(T.out[:, h * H:(h + 1) * H], banks[h][:, 0:H]).then_inc(cp[h], 1)
            queues[h].wait_ge(cp[h], 1)
            queues[h].dma_start(T.y[:, h * H:(h + 1) * H], T.out[:, h * H:(h + 1) * H]).then_inc(st[h], 16)
            queues[h].wait_ge(st[h], 16)
        g.wait_ge(T.sem.sent, n)
        return

    i, l, h = mine[0]
    R, P = rank_at(i, l), rank_at(i, 1 - l)
    order, steps, s = _plan(RA, rounds, i)
    cross = topo.mask(core, P)
    on_only = topo.mask(core, R) & ~cross
    n_in = {k: _count(topo.mask(rank_at(k, l), core)) for k in order[1:]}
    n_in[i] = _count(topo.mask(R, core) & ~topo.mask(R, comb[(rounds[0][i], l)][h]))

    Q = rank_at(rounds[-1][i], 1 - l)
    g.wait_ge(xa[i], n_in[i])
    n = send(Q, _half(T, RAW_X, h), _half(T, i, h), xp[h], topo.mask(core, Q))

    facs = sorted(set(f for op, f in steps if op in ("init", "scale") and f != 1))
    for q, f in enumerate(facs):
        v.memset(T.rs[:, q * H:(q + 1) * H], float(f)).then_inc(T.sem.fill, 1)
    if facs:
        v.wait_ge(T.sem.fill, len(facs))
    banks = [T.pa, T.pb]
    v.wait_ge(xa[order[0]], n_in[order[0]])
    cur = _half(T, order[0], h)
    for done, (op, arg) in enumerate(steps[:-1]):
        if done:
            v.wait_ge(T.sem.vs, done)
        out = banks[done % 2][:, 0:H]
        if op in ("init", "scale"):
            if arg == 1:
                v.tensor_copy(out, cur).then_inc(T.sem.vs, 1)
            else:
                q = facs.index(arg)
                v.tensor_tensor(out, cur, T.rs[:, q * H:(q + 1) * H], AluOpType.mult).then_inc(T.sem.vs, 1)
        else:
            v.wait_ge(xa[arg], n_in[arg])
            v.tensor_tensor(out, cur, _half(T, arg, h), AluOpType.add if op == "add" else AluOpType.subtract
                            ).then_inc(T.sem.vs, 1)
        cur = out
    v.wait_ge(T.sem.vs, len(steps) - 1)
    op, last = steps[-1]
    v.wait_ge(xa[last], n_in[last])
    v.tensor_tensor(T.out[:, 0:H], cur, _half(T, last, h),
                    AluOpType.add if op == "add" else AluOpType.subtract).then_inc(T.sem.vf, 1)
    g.wait_ge(T.sem.vf, 1)
    g.remote_dma_fused([transfer(P, _half(T, CROSS_W, h), T.out[:, 0:H], vcross[h], cross),
                        transfer(R, _half(T, OWN_W, h), T.out[:, 0:H], vown[h], on_only)],
                       local_sem=T.sem.sent)
    n += _count(cross) + _count(on_only)
    g.wait_ge(T.sem.sent, n)
